import numpy as np
import ml_dtypes


def mxq(x, axis, fmt="e4m3"):
    dtype, down = {"e4m3": (ml_dtypes.float8_e4m3fn, 7), "e5m2": (ml_dtypes.float8_e5m2, 14)}[fmt]
    v = np.moveaxis(np.asarray(x, np.float32).astype(ml_dtypes.bfloat16).astype(np.float64), axis, -1)
    blocks = v.reshape(v.shape[:-1] + (-1, 32))
    amax = np.abs(blocks).max(-1, keepdims=True)
    byte = np.maximum(np.where(amax > 0, np.frexp(amax)[1] - 1 + 127, 0) - down, 1)
    scale = np.exp2(byte - 127.0)
    codes = (blocks / scale).astype(np.float32).astype(dtype).astype(np.float64)
    return np.moveaxis((codes * scale).reshape(v.shape), -1, axis)


WIDE = False


def mx_kscale(k):
    if not WIDE:
        return np.ones(k)
    levels = np.array([10, -10, 5, -5, 0])
    if k % 512:
        return np.exp2(np.random.permutation(np.resize(levels, k // 32))).repeat(32)
    a = np.empty((k // 512, 16))
    for p in range(k // 512):
        a[p, :8] = np.random.permutation(np.resize(levels, 8))
        for g in range(8):
            far = levels[np.abs(levels - a[p, g]) >= 10]
            a[p, g + 8] = far[np.random.randint(len(far))]
    return np.exp2(a.ravel()).repeat(32)


def f64(x):
    return np.asarray(x).astype(np.float64)


def striped(idx):
    return np.tile(idx.reshape(-1, 16).T, (8, 1)).astype(np.uint16)


def unstriped(offs):
    return offs[:16].T.reshape(-1).astype(np.int64)


def striped8(idx):
    return np.concatenate([x.reshape(-1, 16).T for x in idx]).astype(np.uint16)


def runs(offs, k):
    lists = np.stack([offs[16 * r : 16 * r + 16].T.reshape(-1) for r in range(8)]).astype(np.int64)
    return lists[np.arange(k) % 512 // 64]


def pack_weight(w):
    k, n = w.shape
    w = f64(np.asarray(w, np.float32).astype(ml_dtypes.bfloat16)).reshape(k // 32, 32, n)
    amax = np.abs(w).max(1)
    byte = np.clip(np.where(amax > 0, np.frexp(amax)[1] - 1 + 127 - 7, 1), 1, 254)
    scaled = (w * np.exp2(127.0 - byte)[:, None, :]).reshape(k, n).astype(np.float32)
    words = np.ascontiguousarray(scaled.reshape(k // 512, 128, 4, n).transpose(0, 1, 3, 2)).astype(ml_dtypes.float8_e4m3fn).view(np.uint8)
    return words, np.ascontiguousarray(byte.astype(np.uint8).reshape(k // 512, 16, n))


def unpack_weight(words, scales):
    g, p, n, _ = words.shape
    vals = np.ascontiguousarray(words).view(ml_dtypes.float8_e4m3fn).astype(np.float64) * np.repeat(np.exp2(scales.astype(np.float64) - 127.0), 8, axis=1)[..., None]
    return vals.transpose(0, 1, 3, 2).reshape(g * 512, n)


def sigmoid(v):
    return 1.0 / (1.0 + np.exp(-np.maximum(v, -700.0)))


K, T, S, N, H = 512, 2048, 512, 512, 512


def setup_inputs():
    n = np.random.standard_normal
    s = mx_kscale(K)[:, None]
    u = mx_kscale(H)
    packed_xT = pack_weight(n((K, T)) * s)
    return {
        "x_words": packed_xT[0],
        "x_scales": packed_xT[1],
        "w1": (n((K, H)) / np.sqrt(K) / s).astype(np.float32),
        "gn": (np.random.uniform(0.5, 1.5, (H, 1)) * u[:, None]).astype(np.float32),
        "w2": (n((H, N)) / np.sqrt(2 * H) / u[:, None]).astype(np.float32),
        "w3": (n((K, N)) / np.sqrt(2 * K) / s).astype(np.float32),
        "sl": np.random.uniform(1.0, 2.0, (N, 1)).astype(np.float32),
        "offs": striped(np.random.permutation(T)[:S]),
        "n1": striped8(np.stack([np.random.permutation(S) for _ in range(8)])),
        "two": striped(np.random.permutation(T)[:S]),
        "n2": striped(np.random.permutation(S)),
    }


def reference(x_words, x_scales, w1, gn, w2, w3, sl, offs, n1, two, n2):
    xq = unpack_weight(x_words, x_scales)[:, unstriped(offs)]
    y = mxq(f64(w1), 0, "e4m3").T @ xq
    z = f64(gn) * (y - (y[np.arange(H)[:, None], runs(n1, H)]))
    x_two = unpack_weight(x_words, x_scales)[:, unstriped(two)]
    h = mxq(f64(w2), 0, "e4m3").T @ mxq(z, 0, "e4m3") + mxq(f64(w3), 0, "e4m3").T @ x_two
    mu = h.mean(axis=1, keepdims=True)
    sg = sigmoid(f64(sl) * (h[:, unstriped(n2)] - mu))
    return (h - mu) * sg

@@ -1,0 +1,181 @@
+from contextlib import ExitStack
+
+import concourse.mybir as mybir
+
+K, T, S, N, H = 512, 2048, 512, 512, 512
+FLOPS = 3 * 2 * 512 * 512 * 512
+
+F32 = mybir.dt.float32
+BF16 = mybir.dt.bfloat16
+I32 = mybir.dt.int32
+U32 = mybir.dt.uint32
+U16 = mybir.dt.uint16
+U8 = mybir.dt.uint8
+FP8X4 = mybir.dt.float8_e4m3fn_x4
+ALU = mybir.AluOpType
+ACT = mybir.ActivationFunctionType
+
+P = 128
+PACK = 4
+TILES = 4
+HALF = S // 2
+PER_COL = 16
+M_SCALAR = 80
+VECTOR_GATHERS = ()
+
+
+def tile_picked_mixindifecn_none_p_kernel(
+    tc, x_words, x_scales, w1, gn, w2, w3, sl, offs, n1, two, n2, out
+):
+    nc = tc.nc
+    with ExitStack() as ctx:
+        keep = ctx.enter_context(tc.tile_pool(name="keep", bufs=1))
+        psum = ctx.enter_context(tc.psum_pool(name="psum", bufs=1))
+
+        def sbuf(name, shape, dtype):
+            return keep.tile(shape, dtype, name=name, align_bytes=64)
+
+        def entries(list_tile, half):
+            cols = HALF // PER_COL
+            return list_tile[:, half * cols : (half + 1) * cols]
+
+        def load_list(name, src):
+            list_tile = keep.tile([P, S // PER_COL], U16, name=name)
+            nc.sync.dma_start(list_tile[:], src)
+            return list_tile
+
+        def load_weight(name, src):
+            raw = sbuf(name, [P, PACK, src.shape[1]], F32)
+            nc.sync.dma_start(raw[:], src.rearrange("(p j) c -> p j c", j=PACK))
+            return raw
+
+        def quantize(name, rounded, width):
+            codes = sbuf(name + "_codes", [P, width], U32)
+            scales = sbuf(name + "_scales", [P, width], U8)
+            nc.vector.quantize_mx(out=codes[:].bitcast(FP8X4), scales=scales[:], in_=rounded)
+            return codes, scales
+
+        def matmul(acc, stationary, moving, start, stop):
+            nc.tensor.matmul_mx(
+                out=acc,
+                lhsT=stationary[0][:].bitcast(FP8X4),
+                lhsT_scale=stationary[1][:],
+                rhs=moving[0][:].bitcast(FP8X4),
+                rhs_scale=moving[1],
+                start=start,
+                stop=stop,
+            )
+
+        x_bytes = sbuf("x_bytes", [P, T], U8)
+        nc.vector.memset(x_bytes[:].bitcast(I32), 0)
+        offs_t = load_list("offs_t", offs)
+        w1_raw = load_weight("w1_raw", w1)
+        for q in range(4):
+            nc.sync.dma_start(
+                x_bytes[32 * q : 32 * q + 4, :].bitcast(I32), x_scales[0, 4 * q : 4 * q + 4, :].bitcast(I32)
+            )
+        x_table = sbuf("x_table", [P, T], U32)
+        nc.sync.dma_start(x_table[:].bitcast(I32), x_words[0].rearrange("p c r -> p (c r)").bitcast(I32))
+        two_t = load_list("two_t", two)
+        gn_t = sbuf("gn_t", [P, PACK], F32)
+        nc.sync.dma_start(gn_t[:], gn.rearrange("(p t) o -> p (t o)", t=PACK))
+        n1_t = load_list("n1_t", n1)
+        w3_raw = load_weight("w3_raw", w3)
+        w2_raw = load_weight("w2_raw", w2)
+        sl_t = sbuf("sl_t", [P, TILES], F32)
+        with nc.allow_non_contiguous_dma(reason="one slope a partition and tile"):
+            nc.sync.dma_start(sl_t[:], sl.rearrange("(a p) o -> p (a o)", p=P))
+        n2_t = load_list("n2_t", n2)
+
+        xa_scales = sbuf("xa_scales", [P, S], U8)
+        nc.vector.tensor_copy(xa_scales[:], x_bytes[:].indirect(offs_t[:]))
+
+        w1_bf = sbuf("w1_bf", [P, H * PACK], BF16)
+        dst = w1_bf[:].rearrange("p (t m j) -> p m j t", t=TILES, j=PACK)
+        src = w1_raw[:].rearrange("p j (m t) -> p m j t", t=TILES)
+        nc.scalar.copy(dst[:, :M_SCALAR], src[:, :M_SCALAR])
+        nc.vector.tensor_copy(dst[:, M_SCALAR:], src[:, M_SCALAR:])
+        w1_q = [quantize("w1_%d" % t, w1_bf[:, t * P * PACK : (t + 1) * P * PACK], P) for t in range(TILES)]
+
+        xa_codes = []
+        for half in range(2):
+            codes = sbuf("xa_codes%d" % half, [P, HALF], U32)
+            nc.vector.tensor_copy(codes[:], x_table[:].indirect(entries(offs_t, half)))
+            xa_codes.append(codes)
+        xb_scales = sbuf("xb_scales", [P, S], U8)
+        nc.vector.tensor_copy(xb_scales[:], x_bytes[:].indirect(two_t[:]))
+        xb_codes = sbuf("xb_codes", [P, S], U32)
+        nc.vector.tensor_copy(xb_codes[:], x_table[:].indirect(two_t[:]))
+
+        y_ps = [psum.tile([P, S], F32, name="y_ps%d" % t) for t in range(TILES)]
+        gy = []
+        for t in range(TILES):
+            for half in range(2):
+                cols = slice(half * HALF, (half + 1) * HALF)
+                matmul(y_ps[t][:, cols], w1_q[t], (xa_codes[half], xa_scales[:, cols]), True, True)
+            window = sbuf("gy%d" % t, [P, S], F32)
+            nc.scalar.activation(window[:], y_ps[t][:], ACT.Copy, scale=gn_t[:, t : t + 1])
+            gy.append(window)
+
+        def round_block(name, raw, a):
+            rounded = sbuf("%s_bf%d" % (name, a), [P, P, PACK], BF16)
+            nc.gpsimd.tensor_scalar(
+                rounded[:], raw[:, :, a * P : (a + 1) * P].rearrange("p j c -> p c j"), 1.0, 0.0, ALU.mult, ALU.add
+            )
+            return rounded[:].rearrange("p c j -> p (c j)")
+
+        w3_bf = [round_block("w3", w3_raw, a) for a in range(TILES)]
+        w2_bf = [round_block("w2", w2_raw, a) for a in range(TILES)]
+
+        z_q = []
+        for half in range(2):
+            cols = slice(half * HALF, (half + 1) * HALF)
+            z_planes = sbuf("z_planes%d" % half, [P, PACK, HALF], BF16)
+            for t in range(TILES):
+                fetched = sbuf("fetched%d_%d" % (half, t), [P, HALF], F32)
+                looked_up = gy[t][:].indirect(entries(n1_t, half))
+                if (t, half) in VECTOR_GATHERS:
+                    nc.vector.tensor_copy(fetched[:], looked_up)
+                else:
+                    nc.scalar.activation(fetched[:], looked_up, ACT.Copy)
+                nc.vector.scalar_tensor_tensor(
+                    z_planes[:, t, :], y_ps[t][:, cols], gn_t[:, t : t + 1], fetched[:], ALU.mult, ALU.subtract
+                )
+            z_bf = sbuf("z_bf%d" % half, [P, HALF * PACK], BF16)
+            nc.vector.tensor_copy(
+                z_bf[:].rearrange("p (c i t) -> p c t i", i=4, t=PACK),
+                z_planes[:].rearrange("p t (c i) -> p c t i", i=4),
+            )
+            z_q.append(quantize("z%d" % half, z_bf[:], HALF))
+
+        coef = sbuf("coef", [P, TILES, 2], F32)
+        nc.vector.memset(coef[:], 1.0 / S)
+        nc.vector.tensor_scalar(coef[:, :, 0], sl_t[:], -1.0 / S, None, ALU.mult)
+
+        h_ps = [psum.tile([P, S], F32, name="h_ps%d" % a) for a in range(TILES)]
+        w3_q = [quantize("w3_%d" % a, w3_bf[a], P) for a in range(TILES)]
+        w2_q = [quantize("w2_%d" % a, w2_bf[a], P) for a in range(TILES)]
+        for a in range(TILES):
+            matmul(h_ps[a][:], w3_q[a], (xb_codes, xb_scales[:]), True, False)
+        for half in range(2):
+            cols = slice(half * HALF, (half + 1) * HALF)
+            for a in range(TILES):
+                matmul(h_ps[a][:, cols], w2_q[a], (z_q[half][0], z_q[half][1][:]), False, half == 1)
+
+        for a in range(TILES):
+            h = sbuf("h%d" % a, [P, S], F32)
+            total = sbuf("total%d" % a, [P, 1], F32)
+            nc.vector.tensor_scalar(h[:], h_ps[a][:], 1.0, None, ALU.mult, ALU.add, accum_out=total[:])
+            stat = sbuf("stat%d" % a, [P, 2], F32)
+            nc.vector.tensor_scalar(stat[:], coef[:, a, :], total[:], None, ALU.mult)
+            for half in range(2):
+                cols = slice(half * HALF, (half + 1) * HALF)
+                gate = sbuf("gate%d_%d" % (a, half), [P, HALF], F32)
+                nc.scalar.activation(
+                    gate[:], h[:].indirect(entries(n2_t, half)), ACT.Sigmoid, bias=stat[:, 0:1], scale=sl_t[:, a : a + 1]
+                )
+                result = sbuf("result%d_%d" % (a, half), [P, HALF], F32)
+                nc.vector.scalar_tensor_tensor(
+                    result[:], h_ps[a][:, cols], stat[:, 1:2], gate[:], ALU.subtract, ALU.mult
+                )
+                nc.sync.dma_start(out[a * P : (a + 1) * P, cols], result[:])

@@ -21,7 +21,7 @@ TILES = 4
 HALF = S // 2
 PER_COL = 16
 M_SCALAR = 80
-VECTOR_GATHERS = ()
+KIB = 1024
 
 
 def tile_picked_mixindifecn_none_p_kernel(
@@ -30,14 +30,19 @@ def tile_picked_mixindifecn_none_p_kernel(
     nc = tc.nc
     with ExitStack() as ctx:
         keep = ctx.enter_context(tc.tile_pool(name="keep", bufs=1))
+        shared = ctx.enter_context(tc.tile_pool(name="shared", bufs=1))
         psum = ctx.enter_context(tc.psum_pool(name="psum", bufs=1))
 
-        def sbuf(name, shape, dtype):
-            return keep.tile(shape, dtype, name=name, align_bytes=64)
+        def sbuf(name, shape, dtype, offset=None, tag=None):
+            if offset is not None:
+                return shared.tile(shape, dtype, name=name, align_bytes=64, offset=offset)
+            return keep.tile(shape, dtype, name=name, tag=tag or name, align_bytes=64)
 
-        def entries(list_tile, half):
-            cols = HALF // PER_COL
-            return list_tile[:, half * cols : (half + 1) * cols]
+        def entries(list_tile, cols):
+            return list_tile[:, cols.start // PER_COL : cols.stop // PER_COL]
+
+        def columns(operand, first, width):
+            return operand[0][:, first : first + width], operand[1][:, first : first + width]
 
         def load_list(name, src):
             list_tile = keep.tile([P, S // PER_COL], U16, name=name)
@@ -49,8 +54,8 @@ def tile_picked_mixindifecn_none_p_kernel(
             nc.sync.dma_start(raw[:], src.rearrange("(p j) c -> p j c", j=PACK))
             return raw
 
-        def quantize(name, rounded, width):
-            codes = sbuf(name + "_codes", [P, width], U32)
+        def quantize(name, rounded, width, offset=None):
+            codes = sbuf(name + "_codes", [P, width], U32, offset=offset)
             scales = sbuf(name + "_scales", [P, width], U8)
             nc.vector.quantize_mx(out=codes[:].bitcast(FP8X4), scales=scales[:], in_=rounded)
             return codes, scales
@@ -58,13 +63,15 @@ def tile_picked_mixindifecn_none_p_kernel(
         def matmul(acc, stationary, moving, start, stop):
             nc.tensor.matmul_mx(
                 out=acc,
-                lhsT=stationary[0][:].bitcast(FP8X4),
-                lhsT_scale=stationary[1][:],
-                rhs=moving[0][:].bitcast(FP8X4),
+                lhsT=stationary[0].bitcast(FP8X4),
+                lhsT_scale=stationary[1],
+                rhs=moving[0].bitcast(FP8X4),
                 rhs_scale=moving[1],
                 start=start,
                 stop=stop,
             )
+
+        halves = [slice(0, HALF), slice(HALF, S)]
 
         x_bytes = sbuf("x_bytes", [P, T], U8)
         nc.vector.memset(x_bytes[:].bitcast(I32), 0)
@@ -77,105 +84,130 @@ def tile_picked_mixindifecn_none_p_kernel(
         x_table = sbuf("x_table", [P, T], U32)
         nc.sync.dma_start(x_table[:].bitcast(I32), x_words[0].rearrange("p c r -> p (c r)").bitcast(I32))
         two_t = load_list("two_t", two)
-        gn_t = sbuf("gn_t", [P, PACK], F32)
+        gn_t = sbuf("gn_t", [P, PACK], F32, offset=10 * KIB)
         nc.sync.dma_start(gn_t[:], gn.rearrange("(p t) o -> p (t o)", t=PACK))
         n1_t = load_list("n1_t", n1)
-        w3_raw = load_weight("w3_raw", w3)
-        w2_raw = load_weight("w2_raw", w2)
+        early_raw = [load_weight(name, w[:, halves[0]]) for name, w in (("w3_raw0", w3), ("w2_raw0", w2))]
         sl_t = sbuf("sl_t", [P, TILES], F32)
         with nc.allow_non_contiguous_dma(reason="one slope a partition and tile"):
             nc.sync.dma_start(sl_t[:], sl.rearrange("(a p) o -> p (a o)", p=P))
         n2_t = load_list("n2_t", n2)
 
-        xa_scales = sbuf("xa_scales", [P, S], U8)
-        nc.vector.tensor_copy(xa_scales[:], x_bytes[:].indirect(offs_t[:]))
-
-        w1_bf = sbuf("w1_bf", [P, H * PACK], BF16)
+        w1_bf = sbuf("w1_bf", [P, H * PACK], BF16, offset=4 * KIB)
         dst = w1_bf[:].rearrange("p (t m j) -> p m j t", t=TILES, j=PACK)
         src = w1_raw[:].rearrange("p j (m t) -> p m j t", t=TILES)
         nc.scalar.copy(dst[:, :M_SCALAR], src[:, :M_SCALAR])
         nc.vector.tensor_copy(dst[:, M_SCALAR:], src[:, M_SCALAR:])
+        xa_scales = sbuf("xa_scales", [P, S], U8)
+        nc.vector.tensor_copy(xa_scales[:], x_bytes[:].indirect(offs_t[:]))
         w1_q = [quantize("w1_%d" % t, w1_bf[:, t * P * PACK : (t + 1) * P * PACK], P) for t in range(TILES)]
 
         xa_codes = []
-        for half in range(2):
-            codes = sbuf("xa_codes%d" % half, [P, HALF], U32)
-            nc.vector.tensor_copy(codes[:], x_table[:].indirect(entries(offs_t, half)))
+        for u in range(2):
+            codes = sbuf("xa_codes%d" % u, [P, HALF], U32, offset=(4 + u) * KIB)
+            nc.vector.tensor_copy(codes[:], x_table[:].indirect(entries(offs_t, halves[u])))
             xa_codes.append(codes)
-        xb_scales = sbuf("xb_scales", [P, S], U8)
+        xb_scales = sbuf("xb_scales", [P, S], U8, offset=6 * KIB)
         nc.vector.tensor_copy(xb_scales[:], x_bytes[:].indirect(two_t[:]))
-        xb_codes = sbuf("xb_codes", [P, S], U32)
+        xb_codes = sbuf("xb_codes", [P, S], U32, offset=7 * KIB)
         nc.vector.tensor_copy(xb_codes[:], x_table[:].indirect(two_t[:]))
 
         y_ps = [psum.tile([P, S], F32, name="y_ps%d" % t) for t in range(TILES)]
         gy = []
+        gy_all = sbuf("gy_all", [P, PACK, S], F32)
         for t in range(TILES):
-            for half in range(2):
-                cols = slice(half * HALF, (half + 1) * HALF)
-                matmul(y_ps[t][:, cols], w1_q[t], (xa_codes[half], xa_scales[:, cols]), True, True)
+            for u in range(2):
+                moving = (xa_codes[u][:], xa_scales[:, halves[u]])
+                matmul(y_ps[t][:, halves[u]], columns(w1_q[t], 0, P), moving, True, True)
             window = sbuf("gy%d" % t, [P, S], F32)
             nc.scalar.activation(window[:], y_ps[t][:], ACT.Copy, scale=gn_t[:, t : t + 1])
+            nc.sync.dma_start(gy_all[:, t, :], window[:])
             gy.append(window)
 
-        def round_block(name, raw, a):
-            rounded = sbuf("%s_bf%d" % (name, a), [P, P, PACK], BF16)
-            nc.gpsimd.tensor_scalar(
-                rounded[:], raw[:, :, a * P : (a + 1) * P].rearrange("p j c -> p c j"), 1.0, 0.0, ALU.mult, ALU.add
-            )
-            return rounded[:].rearrange("p c j -> p (c j)")
+        late_raw = sbuf("late_raw", [P, 2, PACK, HALF], F32, offset=10 * KIB)
+        for i, w in enumerate((w3, w2)):
+            nc.sync.dma_start(late_raw[:, i], w[:, halves[1]].rearrange("(p j) c -> p j c", j=PACK))
 
-        w3_bf = [round_block("w3", w3_raw, a) for a in range(TILES)]
-        w2_bf = [round_block("w2", w2_raw, a) for a in range(TILES)]
+        def round_weight(copy, rounded, raw):
+            copy(rounded.rearrange("p (c i j) -> p c j i", i=4, j=PACK), raw.rearrange("p j (c i) -> p c j i", i=4))
 
-        z_q = []
-        for half in range(2):
-            cols = slice(half * HALF, (half + 1) * HALF)
-            z_planes = sbuf("z_planes%d" % half, [P, PACK, HALF], BF16)
-            for t in range(TILES):
-                fetched = sbuf("fetched%d_%d" % (half, t), [P, HALF], F32)
-                looked_up = gy[t][:].indirect(entries(n1_t, half))
-                if (t, half) in VECTOR_GATHERS:
-                    nc.vector.tensor_copy(fetched[:], looked_up)
-                else:
-                    nc.scalar.activation(fetched[:], looked_up, ACT.Copy)
-                nc.vector.scalar_tensor_tensor(
-                    z_planes[:, t, :], y_ps[t][:, cols], gn_t[:, t : t + 1], fetched[:], ALU.mult, ALU.subtract
-                )
-            z_bf = sbuf("z_bf%d" % half, [P, HALF * PACK], BF16)
-            nc.vector.tensor_copy(
-                z_bf[:].rearrange("p (c i t) -> p c t i", i=4, t=PACK),
-                z_planes[:].rearrange("p t (c i) -> p c t i", i=4),
-            )
-            z_q.append(quantize("z%d" % half, z_bf[:], HALF))
+        fetched = [sbuf("fetched%d" % u, [P, PACK, HALF], F32) for u in range(2)]
+        nc.vector.tensor_copy(fetched[0][:, 0, :], gy[0][:].indirect(entries(n1_t, halves[0])))
+
+        early_bf = sbuf("early_bf", [P, 2 * HALF * PACK], BF16, offset=KIB)
+        for i in range(2):
+            round_weight(nc.vector.tensor_copy, early_bf[:, i * HALF * PACK : (i + 1) * HALF * PACK], early_raw[i][:])
+        early_q = quantize("early", early_bf[:], S)
+        w3_q = [columns(early_q, 0, HALF)]
+        w2_q = [columns(early_q, HALF, HALF)]
 
         coef = sbuf("coef", [P, TILES, 2], F32)
-        nc.vector.memset(coef[:], 1.0 / S)
-        nc.vector.tensor_scalar(coef[:, :, 0], sl_t[:], -1.0 / S, None, ALU.mult)
+        nc.gpsimd.memset(coef[:], 1.0 / S)
+        nc.gpsimd.tensor_scalar(coef[:, :, 0], sl_t[:], -1.0 / S, 0.0, ALU.mult, ALU.add)
+
+        z_q = []
+        for u in range(2):
+            for t in range(1 - u, TILES):
+                nc.scalar.activation(fetched[u][:, t, :], gy[t][:].indirect(entries(n1_t, halves[u])), ACT.Copy)
+            z_bf = sbuf("z_bf%d" % u, [P, HALF * PACK], BF16)
+            nc.vector.tensor_tensor(
+                z_bf[:].rearrange("p (c i t) -> p c t i", i=4, t=PACK),
+                gy_all[:, :, halves[u]].rearrange("p t (c i) -> p c t i", i=4),
+                fetched[u][:].rearrange("p t (c i) -> p c t i", i=4),
+                ALU.subtract,
+            )
+            z_q.append(quantize("z%d" % u, z_bf[:], HALF))
+        w3_late = sbuf("w3_late", [P, HALF * PACK], BF16, tag="gy2")
+        round_weight(nc.scalar.copy, w3_late[:], late_raw[:, 0])
+        w2_late = sbuf("w2_late", [P, HALF * PACK], BF16, tag="z_bf1")
+        round_weight(nc.vector.tensor_copy, w2_late[:], late_raw[:, 1])
 
         h_ps = [psum.tile([P, S], F32, name="h_ps%d" % a) for a in range(TILES)]
-        w3_q = [quantize("w3_%d" % a, w3_bf[a], P) for a in range(TILES)]
-        w2_q = [quantize("w2_%d" % a, w2_bf[a], P) for a in range(TILES)]
-        for a in range(TILES):
-            matmul(h_ps[a][:], w3_q[a], (xb_codes, xb_scales[:]), True, False)
-        for half in range(2):
-            cols = slice(half * HALF, (half + 1) * HALF)
-            for a in range(TILES):
-                matmul(h_ps[a][:, cols], w2_q[a], (z_q[half][0], z_q[half][1][:]), False, half == 1)
 
-        for a in range(TILES):
-            h = sbuf("h%d" % a, [P, S], F32)
-            total = sbuf("total%d" % a, [P, 1], F32)
-            nc.vector.tensor_scalar(h[:], h_ps[a][:], 1.0, None, ALU.mult, ALU.add, accum_out=total[:])
-            stat = sbuf("stat%d" % a, [P, 2], F32)
-            nc.vector.tensor_scalar(stat[:], coef[:, a, :], total[:], None, ALU.mult)
-            for half in range(2):
-                cols = slice(half * HALF, (half + 1) * HALF)
-                gate = sbuf("gate%d_%d" % (a, half), [P, HALF], F32)
+        def second_layer(pair):
+            for b in range(2):
+                moving = columns((xb_codes, xb_scales), 0, S)
+                matmul(h_ps[2 * pair + b][:], columns(w3_q[pair], b * P, P), moving, True, False)
+            for u in range(2):
+                for b in range(2):
+                    stationary = columns(w2_q[pair], b * P, P)
+                    matmul(h_ps[2 * pair + b][:, halves[u]], stationary, columns(z_q[u], 0, HALF), False, u == 1)
+
+        h, stat = {}, {}
+
+        def leave_psum(a):
+            h[a] = sbuf("h%d" % a, [P, S], F32)
+            total = sbuf("total%d" % a, [P, 32], F32, offset=19 * KIB - 64 if a == 0 else None)
+            nc.vector.tensor_scalar(h[a][:], h_ps[a][:], 1.0, None, ALU.mult, ALU.add, accum_out=total[:, 0:1])
+            stat[a] = sbuf("stat%d" % a, [P, 2], F32)
+            nc.gpsimd.tensor_scalar(stat[a][:], coef[:, a, :], total[:, 0:1], 0.0, ALU.mult, ALU.add)
+
+        def gate_and_store(a):
+            gate = sbuf("gate%d" % a, [P, S], F32)
+            for u in range(2):
                 nc.scalar.activation(
-                    gate[:], h[:].indirect(entries(n2_t, half)), ACT.Sigmoid, bias=stat[:, 0:1], scale=sl_t[:, a : a + 1]
+                    gate[:, halves[u]],
+                    h[a][:].indirect(entries(n2_t, halves[u])),
+                    ACT.Sigmoid,
+                    bias=stat[a][:, 0:1],
+                    scale=sl_t[:, a : a + 1],
                 )
-                result = sbuf("result%d_%d" % (a, half), [P, HALF], F32)
+            result = sbuf("result%d" % a, [P, S], F32)
+            for cols in halves if a == TILES - 1 else [slice(0, S)]:
                 nc.vector.scalar_tensor_tensor(
-                    result[:], h_ps[a][:, cols], stat[:, 1:2], gate[:], ALU.subtract, ALU.mult
+                    result[:, cols], h_ps[a][:, cols], stat[a][:, 1:2], gate[:, cols], ALU.subtract, ALU.mult
                 )
-                nc.sync.dma_start(out[a * P : (a + 1) * P, cols], result[:])
+                nc.sync.dma_start(out[a * P : (a + 1) * P, cols], result[:, cols])
+
+        second_layer(0)
+        leave_psum(0)
+        w3_q.append(quantize("w3_late", w3_late[:], HALF, offset=18 * KIB))
+        w2_q.append(quantize("w2_late", w2_late[:], HALF, offset=19 * KIB))
+        second_layer(1)
+        leave_psum(1)
+        leave_psum(2)
+        gate_and_store(0)
+        leave_psum(3)
+        gate_and_store(1)
+        gate_and_store(2)
+        gate_and_store(3)

@@ -22,6 +22,7 @@ HALF = S // 2
 PER_COL = 16
 M_SCALAR = 80
 KIB = 1024
+VECTOR_GATHERS = ((0, 0), (1, 0), (0, 1))
 
 
 def tile_picked_mixindifecn_none_p_kernel(
@@ -76,40 +77,54 @@ def tile_picked_mixindifecn_none_p_kernel(
         x_bytes = sbuf("x_bytes", [P, T], U8)
         nc.vector.memset(x_bytes[:].bitcast(I32), 0)
         offs_t = load_list("offs_t", offs)
-        w1_raw = load_weight("w1_raw", w1)
+        two_t = load_list("two_t", two)
+        w1_raw = sbuf("w1_raw", [P, PACK, H], F32)
+        w1_rows = w1.rearrange("(p j) c -> p j c", j=PACK)
+        nc.sync.dma_start(w1_raw[:, :2], w1_rows[:, :2])
         for q in range(4):
             nc.sync.dma_start(
                 x_bytes[32 * q : 32 * q + 4, :].bitcast(I32), x_scales[0, 4 * q : 4 * q + 4, :].bitcast(I32)
             )
+        nc.sync.dma_start(w1_raw[:, 2:], w1_rows[:, 2:])
         x_table = sbuf("x_table", [P, T], U32)
         nc.sync.dma_start(x_table[:].bitcast(I32), x_words[0].rearrange("p c r -> p (c r)").bitcast(I32))
-        two_t = load_list("two_t", two)
-        gn_t = sbuf("gn_t", [P, PACK], F32, offset=10 * KIB)
+        gn_t = sbuf("gn_t", [P, PACK], F32)
         nc.sync.dma_start(gn_t[:], gn.rearrange("(p t) o -> p (t o)", t=PACK))
         n1_t = load_list("n1_t", n1)
-        early_raw = [load_weight(name, w[:, halves[0]]) for name, w in (("w3_raw0", w3), ("w2_raw0", w2))]
+        w3_raw, w2_raw = [], []
+        for u in range(2):
+            w3_raw.append(load_weight("w3_raw%d" % u, w3[:, halves[u]]))
+            w2_raw.append(load_weight("w2_raw%d" % u, w2[:, halves[u]]))
         sl_t = sbuf("sl_t", [P, TILES], F32)
         with nc.allow_non_contiguous_dma(reason="one slope a partition and tile"):
             nc.sync.dma_start(sl_t[:], sl.rearrange("(a p) o -> p (a o)", p=P))
         n2_t = load_list("n2_t", n2)
+
+        coef = sbuf("coef", [P, TILES, 2], F32)
+        nc.gpsimd.memset(coef[:], 1.0 / S)
+        h = [sbuf("h%d" % a, [P, S if a == TILES - 1 else 2 * S], F32) for a in range(TILES)]
+        nc.gpsimd.memset(h[0][:, S:], 0.0)
+        for a in range(1, TILES - 1):
+            nc.scalar.activation(h[a][:, S:], h[0][:, S:], ACT.Sigmoid)
+
+        xa_scales = sbuf("xa_scales", [P, S], U8)
+        nc.vector.tensor_copy(xa_scales[:], x_bytes[:].indirect(offs_t[:]))
+        xb_scales = sbuf("xb_scales", [P, S], U8)
+        nc.vector.tensor_copy(xb_scales[:], x_bytes[:].indirect(two_t[:]))
 
         w1_bf = sbuf("w1_bf", [P, H * PACK], BF16, offset=4 * KIB)
         dst = w1_bf[:].rearrange("p (t m j) -> p m j t", t=TILES, j=PACK)
         src = w1_raw[:].rearrange("p j (m t) -> p m j t", t=TILES)
         nc.scalar.copy(dst[:, :M_SCALAR], src[:, :M_SCALAR])
         nc.vector.tensor_copy(dst[:, M_SCALAR:], src[:, M_SCALAR:])
-        xa_scales = sbuf("xa_scales", [P, S], U8)
-        nc.vector.tensor_copy(xa_scales[:], x_bytes[:].indirect(offs_t[:]))
-        w1_q = [quantize("w1_%d" % t, w1_bf[:, t * P * PACK : (t + 1) * P * PACK], P) for t in range(TILES)]
+        w1_q = quantize("w1", w1_bf[:], H)
 
         xa_codes = []
         for u in range(2):
             codes = sbuf("xa_codes%d" % u, [P, HALF], U32, offset=(4 + u) * KIB)
             nc.vector.tensor_copy(codes[:], x_table[:].indirect(entries(offs_t, halves[u])))
             xa_codes.append(codes)
-        xb_scales = sbuf("xb_scales", [P, S], U8, offset=6 * KIB)
-        nc.vector.tensor_copy(xb_scales[:], x_bytes[:].indirect(two_t[:]))
-        xb_codes = sbuf("xb_codes", [P, S], U32, offset=7 * KIB)
+        xb_codes = sbuf("xb_codes", [P, S], U32, offset=6 * KIB)
         nc.vector.tensor_copy(xb_codes[:], x_table[:].indirect(two_t[:]))
 
         y_ps = [psum.tile([P, S], F32, name="y_ps%d" % t) for t in range(TILES)]
@@ -118,38 +133,45 @@ def tile_picked_mixindifecn_none_p_kernel(
         for t in range(TILES):
             for u in range(2):
                 moving = (xa_codes[u][:], xa_scales[:, halves[u]])
-                matmul(y_ps[t][:, halves[u]], columns(w1_q[t], 0, P), moving, True, True)
+                matmul(y_ps[t][:, halves[u]], columns(w1_q, t * P, P), moving, True, True)
             window = sbuf("gy%d" % t, [P, S], F32)
             nc.scalar.activation(window[:], y_ps[t][:], ACT.Copy, scale=gn_t[:, t : t + 1])
-            nc.sync.dma_start(gy_all[:, t, :], window[:])
+            if t < 2:
+                nc.sync.dma_start(gy_all[:, t, :], window[:])
             gy.append(window)
-
-        late_raw = sbuf("late_raw", [P, 2, PACK, HALF], F32, offset=10 * KIB)
-        for i, w in enumerate((w3, w2)):
-            nc.sync.dma_start(late_raw[:, i], w[:, halves[1]].rearrange("(p j) c -> p j c", j=PACK))
 
         def round_weight(copy, rounded, raw):
             copy(rounded.rearrange("p (c i j) -> p c j i", i=4, j=PACK), raw.rearrange("p j (c i) -> p c j i", i=4))
 
         fetched = [sbuf("fetched%d" % u, [P, PACK, HALF], F32) for u in range(2)]
-        nc.vector.tensor_copy(fetched[0][:, 0, :], gy[0][:].indirect(entries(n1_t, halves[0])))
+        for t, u in VECTOR_GATHERS:
+            nc.vector.tensor_copy(fetched[u][:, t, :], gy[t][:].indirect(entries(n1_t, halves[u])))
 
-        early_bf = sbuf("early_bf", [P, 2 * HALF * PACK], BF16, offset=KIB)
-        for i in range(2):
-            round_weight(nc.vector.tensor_copy, early_bf[:, i * HALF * PACK : (i + 1) * HALF * PACK], early_raw[i][:])
-        early_q = quantize("early", early_bf[:], S)
+        for t in range(2, TILES):
+            nc.vector.tensor_copy(gy_all[:, t, :], gy[t][:])
+
+        def round_on_gpsimd(name, raws):
+            rounded = sbuf(name, [P, 2 * len(raws), P, PACK], BF16)
+            for b in range(2 * len(raws)):
+                block = raws[b // 2][:, :, b % 2 * P : (b % 2 + 1) * P].rearrange("p j c -> p c j")
+                nc.gpsimd.tensor_scalar(rounded[:, b], block, 1.0, 0.0, ALU.mult, ALU.add)
+            return rounded[:].rearrange("p b c j -> p (b c j)")
+
+        early_bf = round_on_gpsimd("early_bf", [w3_raw[0], w2_raw[0]])
+        w3_late = round_on_gpsimd("w3_late", [w3_raw[1]])
+        early_q = quantize("early", early_bf, S)
         w3_q = [columns(early_q, 0, HALF)]
         w2_q = [columns(early_q, HALF, HALF)]
 
-        coef = sbuf("coef", [P, TILES, 2], F32)
-        nc.gpsimd.memset(coef[:], 1.0 / S)
         nc.gpsimd.tensor_scalar(coef[:, :, 0], sl_t[:], -1.0 / S, 0.0, ALU.mult, ALU.add)
 
         z_q = []
         for u in range(2):
-            for t in range(1 - u, TILES):
-                nc.scalar.activation(fetched[u][:, t, :], gy[t][:].indirect(entries(n1_t, halves[u])), ACT.Copy)
-            z_bf = sbuf("z_bf%d" % u, [P, HALF * PACK], BF16)
+            for t in range(TILES):
+                if (t, u) not in VECTOR_GATHERS:
+                    nc.scalar.activation(fetched[u][:, t, :], gy[t][:].indirect(entries(n1_t, halves[u])), ACT.Copy)
+            place = {"offset": 8 * KIB} if u == 1 else {"tag": "early_bf"}
+            z_bf = sbuf("z_bf%d" % u, [P, HALF * PACK], BF16, **place)
             nc.vector.tensor_tensor(
                 z_bf[:].rearrange("p (c i t) -> p c t i", i=4, t=PACK),
                 gy_all[:, :, halves[u]].rearrange("p t (c i) -> p c t i", i=4),
@@ -157,53 +179,58 @@ def tile_picked_mixindifecn_none_p_kernel(
                 ALU.subtract,
             )
             z_q.append(quantize("z%d" % u, z_bf[:], HALF))
-        w3_late = sbuf("w3_late", [P, HALF * PACK], BF16, tag="gy2")
-        round_weight(nc.scalar.copy, w3_late[:], late_raw[:, 0])
-        w2_late = sbuf("w2_late", [P, HALF * PACK], BF16, tag="z_bf1")
-        round_weight(nc.vector.tensor_copy, w2_late[:], late_raw[:, 1])
+        w2_late = sbuf("w2_late", [P, HALF * PACK], BF16, tag="gy2")
+        round_weight(nc.scalar.copy, w2_late[:], w2_raw[1][:])
+
+        w3_q.append(quantize("w3_late", w3_late, HALF, offset=8 * KIB))
+        w2_q.append(quantize("w2_late", w2_late[:], HALF, offset=9 * KIB))
 
         h_ps = [psum.tile([P, S], F32, name="h_ps%d" % a) for a in range(TILES)]
 
-        def second_layer(pair):
-            for b in range(2):
-                moving = columns((xb_codes, xb_scales), 0, S)
-                matmul(h_ps[2 * pair + b][:], columns(w3_q[pair], b * P, P), moving, True, False)
-            for u in range(2):
-                for b in range(2):
-                    stationary = columns(w2_q[pair], b * P, P)
-                    matmul(h_ps[2 * pair + b][:, halves[u]], stationary, columns(z_q[u], 0, HALF), False, u == 1)
+        def tokens_pass(a):
+            moving = columns((xb_codes, xb_scales), 0, S)
+            matmul(h_ps[a][:], columns(w3_q[a // 2], a % 2 * P, P), moving, True, False)
 
-        h, stat = {}, {}
+        def z_pass(a, u):
+            stationary = columns(w2_q[a // 2], a % 2 * P, P)
+            matmul(h_ps[a][:, halves[u]], stationary, columns(z_q[u], 0, HALF), False, u == 1)
+
+        stat = {}
 
         def leave_psum(a):
-            h[a] = sbuf("h%d" % a, [P, S], F32)
-            total = sbuf("total%d" % a, [P, 32], F32, offset=19 * KIB - 64 if a == 0 else None)
-            nc.vector.tensor_scalar(h[a][:], h_ps[a][:], 1.0, None, ALU.mult, ALU.add, accum_out=total[:, 0:1])
+            total = sbuf("total%d" % a, [P, 1], F32)
             stat[a] = sbuf("stat%d" % a, [P, 2], F32)
-            nc.gpsimd.tensor_scalar(stat[a][:], coef[:, a, :], total[:, 0:1], 0.0, ALU.mult, ALU.add)
+            nc.vector.tensor_scalar(h[a][:, :S], h_ps[a][:], 1.0, None, ALU.mult, ALU.add, accum_out=total[:])
+            nc.gpsimd.tensor_scalar(stat[a][:], coef[:, a, :], total[:], 0.0, ALU.mult, ALU.add)
 
         def gate_and_store(a):
+            pieces = halves if a == TILES - 1 else [slice(0, S)]
             gate = sbuf("gate%d" % a, [P, S], F32)
-            for u in range(2):
+            for cols in pieces:
                 nc.scalar.activation(
-                    gate[:, halves[u]],
-                    h[a][:].indirect(entries(n2_t, halves[u])),
+                    gate[:, cols],
+                    h[a][:].indirect(entries(n2_t, cols)),
                     ACT.Sigmoid,
                     bias=stat[a][:, 0:1],
                     scale=sl_t[:, a : a + 1],
                 )
-            result = sbuf("result%d" % a, [P, S], F32)
-            for cols in halves if a == TILES - 1 else [slice(0, S)]:
+            result = sbuf("result%d" % a, [P, S], F32, tag="total%d" % (a + 2) if a < 2 else None)
+            for cols in pieces:
                 nc.vector.scalar_tensor_tensor(
                     result[:, cols], h_ps[a][:, cols], stat[a][:, 1:2], gate[:, cols], ALU.subtract, ALU.mult
                 )
                 nc.sync.dma_start(out[a * P : (a + 1) * P, cols], result[:, cols])
 
-        second_layer(0)
+        for a in range(2):
+            tokens_pass(a)
+        for u in range(2):
+            for a in range(2):
+                z_pass(a, u)
         leave_psum(0)
-        w3_q.append(quantize("w3_late", w3_late[:], HALF, offset=18 * KIB))
-        w2_q.append(quantize("w2_late", w2_late[:], HALF, offset=19 * KIB))
-        second_layer(1)
+        for a in range(2, TILES):
+            tokens_pass(a)
+            for u in range(2):
+                z_pass(a, u)
         leave_psum(1)
         leave_psum(2)
         gate_and_store(0)

from contextlib import ExitStack

import concourse.mybir as mybir

K, T, S, N, H = 512, 2048, 512, 512, 512
FLOPS = 3 * 2 * 512 * 512 * 512

F32 = mybir.dt.float32
BF16 = mybir.dt.bfloat16
I32 = mybir.dt.int32
U32 = mybir.dt.uint32
U16 = mybir.dt.uint16
U8 = mybir.dt.uint8
FP8X4 = mybir.dt.float8_e4m3fn_x4
ALU = mybir.AluOpType
ACT = mybir.ActivationFunctionType

P = 128
PACK = 4
TILES = 4
HALF = S // 2
PER_COL = 16
M_SCALAR = 80
KIB = 1024
VECTOR_GATHERS = ((0, 0), (1, 0), (0, 1))


def tile_picked_mixindifecn_none_p_kernel(
    tc, x_words, x_scales, w1, gn, w2, w3, sl, offs, n1, two, n2, out
):
    nc = tc.nc
    with ExitStack() as ctx:
        keep = ctx.enter_context(tc.tile_pool(name="keep", bufs=1))
        shared = ctx.enter_context(tc.tile_pool(name="shared", bufs=1))
        psum = ctx.enter_context(tc.psum_pool(name="psum", bufs=1))

        def sbuf(name, shape, dtype, offset=None, tag=None):
            if offset is not None:
                return shared.tile(shape, dtype, name=name, align_bytes=64, offset=offset)
            return keep.tile(shape, dtype, name=name, tag=tag or name, align_bytes=64)

        def entries(list_tile, cols):
            return list_tile[:, cols.start // PER_COL : cols.stop // PER_COL]

        def columns(operand, first, width):
            return operand[0][:, first : first + width], operand[1][:, first : first + width]

        def load_list(name, src):
            list_tile = keep.tile([P, S // PER_COL], U16, name=name)
            nc.sync.dma_start(list_tile[:], src)
            return list_tile

        def load_weight(name, src):
            raw = sbuf(name, [P, PACK, src.shape[1]], F32)
            nc.sync.dma_start(raw[:], src.rearrange("(p j) c -> p j c", j=PACK))
            return raw

        def quantize(name, rounded, width, offset=None):
            codes = sbuf(name + "_codes", [P, width], U32, offset=offset)
            scales = sbuf(name + "_scales", [P, width], U8)
            nc.vector.quantize_mx(out=codes[:].bitcast(FP8X4), scales=scales[:], in_=rounded)
            return codes, scales

        def matmul(acc, stationary, moving, start, stop):
            nc.tensor.matmul_mx(
                out=acc,
                lhsT=stationary[0].bitcast(FP8X4),
                lhsT_scale=stationary[1],
                rhs=moving[0].bitcast(FP8X4),
                rhs_scale=moving[1],
                start=start,
                stop=stop,
            )

        halves = [slice(0, HALF), slice(HALF, S)]

        x_bytes = sbuf("x_bytes", [P, T], U8)
        nc.vector.memset(x_bytes[:].bitcast(I32), 0)
        offs_t = load_list("offs_t", offs)
        two_t = load_list("two_t", two)
        w1_raw = sbuf("w1_raw", [P, PACK, H], F32)
        w1_rows = w1.rearrange("(p j) c -> p j c", j=PACK)
        nc.sync.dma_start(w1_raw[:, :2], w1_rows[:, :2])
        for q in range(4):
            nc.sync.dma_start(
                x_bytes[32 * q : 32 * q + 4, :].bitcast(I32), x_scales[0, 4 * q : 4 * q + 4, :].bitcast(I32)
            )
        nc.sync.dma_start(w1_raw[:, 2:], w1_rows[:, 2:])
        x_table = sbuf("x_table", [P, T], U32)
        nc.sync.dma_start(x_table[:].bitcast(I32), x_words[0].rearrange("p c r -> p (c r)").bitcast(I32))
        gn_t = sbuf("gn_t", [P, PACK], F32)
        nc.sync.dma_start(gn_t[:], gn.rearrange("(p t) o -> p (t o)", t=PACK))
        n1_t = load_list("n1_t", n1)
        w3_raw, w2_raw = [], []
        for u in range(2):
            w3_raw.append(load_weight("w3_raw%d" % u, w3[:, halves[u]]))
            w2_raw.append(load_weight("w2_raw%d" % u, w2[:, halves[u]]))
        sl_t = sbuf("sl_t", [P, TILES], F32)
        with nc.allow_non_contiguous_dma(reason="one slope a partition and tile"):
            nc.sync.dma_start(sl_t[:], sl.rearrange("(a p) o -> p (a o)", p=P))
        n2_t = load_list("n2_t", n2)

        coef = sbuf("coef", [P, TILES, 2], F32)
        nc.gpsimd.memset(coef[:], 1.0 / S)
        h = [sbuf("h%d" % a, [P, S if a == TILES - 1 else 2 * S], F32) for a in range(TILES)]
        nc.gpsimd.memset(h[0][:, S:], 0.0)
        for a in range(1, TILES - 1):
            nc.scalar.activation(h[a][:, S:], h[0][:, S:], ACT.Sigmoid)

        xa_scales = sbuf("xa_scales", [P, S], U8)
        nc.vector.tensor_copy(xa_scales[:], x_bytes[:].indirect(offs_t[:]))
        xb_scales = sbuf("xb_scales", [P, S], U8)
        nc.vector.tensor_copy(xb_scales[:], x_bytes[:].indirect(two_t[:]))

        w1_bf = sbuf("w1_bf", [P, H * PACK], BF16, offset=4 * KIB)
        dst = w1_bf[:].rearrange("p (t m j) -> p m j t", t=TILES, j=PACK)
        src = w1_raw[:].rearrange("p j (m t) -> p m j t", t=TILES)
        nc.scalar.copy(dst[:, :M_SCALAR], src[:, :M_SCALAR])
        nc.vector.tensor_copy(dst[:, M_SCALAR:], src[:, M_SCALAR:])
        w1_q = quantize("w1", w1_bf[:], H)

        xa_codes = []
        for u in range(2):
            codes = sbuf("xa_codes%d" % u, [P, HALF], U32, offset=(4 + u) * KIB)
            nc.vector.tensor_copy(codes[:], x_table[:].indirect(entries(offs_t, halves[u])))
            xa_codes.append(codes)
        xb_codes = sbuf("xb_codes", [P, S], U32, offset=6 * KIB)
        nc.vector.tensor_copy(xb_codes[:], x_table[:].indirect(two_t[:]))

        y_ps = [psum.tile([P, S], F32, name="y_ps%d" % t) for t in range(TILES)]
        gy = []
        gy_all = sbuf("gy_all", [P, PACK, S], F32)
        for t in range(TILES):
            for u in range(2):
                moving = (xa_codes[u][:], xa_scales[:, halves[u]])
                matmul(y_ps[t][:, halves[u]], columns(w1_q, t * P, P), moving, True, True)
            window = sbuf("gy%d" % t, [P, S], F32)
            nc.scalar.activation(window[:], y_ps[t][:], ACT.Copy, scale=gn_t[:, t : t + 1])
            if t < 2:
                nc.sync.dma_start(gy_all[:, t, :], window[:])
            gy.append(window)

        def round_weight(copy, rounded, raw):
            copy(rounded.rearrange("p (c i j) -> p c j i", i=4, j=PACK), raw.rearrange("p j (c i) -> p c j i", i=4))

        fetched = [sbuf("fetched%d" % u, [P, PACK, HALF], F32) for u in range(2)]
        for t, u in VECTOR_GATHERS:
            nc.vector.tensor_copy(fetched[u][:, t, :], gy[t][:].indirect(entries(n1_t, halves[u])))

        for t in range(2, TILES):
            nc.vector.tensor_copy(gy_all[:, t, :], gy[t][:])

        def round_on_gpsimd(name, raws):
            rounded = sbuf(name, [P, 2 * len(raws), P, PACK], BF16)
            for b in range(2 * len(raws)):
                block = raws[b // 2][:, :, b % 2 * P : (b % 2 + 1) * P].rearrange("p j c -> p c j")
                nc.gpsimd.tensor_scalar(rounded[:, b], block, 1.0, 0.0, ALU.mult, ALU.add)
            return rounded[:].rearrange("p b c j -> p (b c j)")

        early_bf = round_on_gpsimd("early_bf", [w3_raw[0], w2_raw[0]])
        w3_late = round_on_gpsimd("w3_late", [w3_raw[1]])
        early_q = quantize("early", early_bf, S)
        w3_q = [columns(early_q, 0, HALF)]
        w2_q = [columns(early_q, HALF, HALF)]

        nc.gpsimd.tensor_scalar(coef[:, :, 0], sl_t[:], -1.0 / S, 0.0, ALU.mult, ALU.add)

        z_q = []
        for u in range(2):
            for t in range(TILES):
                if (t, u) not in VECTOR_GATHERS:
                    nc.scalar.activation(fetched[u][:, t, :], gy[t][:].indirect(entries(n1_t, halves[u])), ACT.Copy)
            place = {"offset": 8 * KIB} if u == 1 else {"tag": "early_bf"}
            z_bf = sbuf("z_bf%d" % u, [P, HALF * PACK], BF16, **place)
            nc.vector.tensor_tensor(
                z_bf[:].rearrange("p (c i t) -> p c t i", i=4, t=PACK),
                gy_all[:, :, halves[u]].rearrange("p t (c i) -> p c t i", i=4),
                fetched[u][:].rearrange("p t (c i) -> p c t i", i=4),
                ALU.subtract,
            )
            z_q.append(quantize("z%d" % u, z_bf[:], HALF))
        w2_late = sbuf("w2_late", [P, HALF * PACK], BF16, tag="gy2")
        round_weight(nc.scalar.copy, w2_late[:], w2_raw[1][:])

        w3_q.append(quantize("w3_late", w3_late, HALF, offset=8 * KIB))
        w2_q.append(quantize("w2_late", w2_late[:], HALF, offset=9 * KIB))

        h_ps = [psum.tile([P, S], F32, name="h_ps%d" % a) for a in range(TILES)]

        def tokens_pass(a):
            moving = columns((xb_codes, xb_scales), 0, S)
            matmul(h_ps[a][:], columns(w3_q[a // 2], a % 2 * P, P), moving, True, False)

        def z_pass(a, u):
            stationary = columns(w2_q[a // 2], a % 2 * P, P)
            matmul(h_ps[a][:, halves[u]], stationary, columns(z_q[u], 0, HALF), False, u == 1)

        stat = {}

        def leave_psum(a):
            total = sbuf("total%d" % a, [P, 1], F32)
            stat[a] = sbuf("stat%d" % a, [P, 2], F32)
            nc.vector.tensor_scalar(h[a][:, :S], h_ps[a][:], 1.0, None, ALU.mult, ALU.add, accum_out=total[:])
            nc.gpsimd.tensor_scalar(stat[a][:], coef[:, a, :], total[:], 0.0, ALU.mult, ALU.add)

        def gate_and_store(a):
            pieces = halves if a == TILES - 1 else [slice(0, S)]
            gate = sbuf("gate%d" % a, [P, S], F32)
            for cols in pieces:
                nc.scalar.activation(
                    gate[:, cols],
                    h[a][:].indirect(entries(n2_t, cols)),
                    ACT.Sigmoid,
                    bias=stat[a][:, 0:1],
                    scale=sl_t[:, a : a + 1],
                )
            result = sbuf("result%d" % a, [P, S], F32, tag="total%d" % (a + 2) if a < 2 else None)
            for cols in pieces:
                nc.vector.scalar_tensor_tensor(
                    result[:, cols], h_ps[a][:, cols], stat[a][:, 1:2], gate[:, cols], ALU.subtract, ALU.mult
                )
                nc.sync.dma_start(out[a * P : (a + 1) * P, cols], result[:, cols])

        for a in range(2):
            tokens_pass(a)
        for u in range(2):
            for a in range(2):
                z_pass(a, u)
        leave_psum(0)
        for a in range(2, TILES):
            tokens_pass(a)
            for u in range(2):
                z_pass(a, u)
        leave_psum(1)
        leave_psum(2)
        gate_and_store(0)
        leave_psum(3)
        gate_and_store(1)
        gate_and_store(2)
        gate_and_store(3)
